import numpy as np, ml_dtypes
CORES = [6,10,22,26,38,42,54,58]
N = 8
T = 8
ROUTE = [[[7,5],[5,4],[3,5],[5,7],[4,5],[5,3],[1,5],[1,4]],[[3,7],[5,0],[1,5],[5,0],[3,6],[5,4],[5,3],[4,5]],[[5,7],[5,4],[5,1],[1,5],[2,5],[4,3],[5,1],[5,4]],[[3,5],[5,4],[5,4],[4,1],[0,5],[6,0],[4,5],[1,5]],[[2,3],[6,0],[5,1],[5,6],[0,5],[0,5],[5,4],[4,5]],[[3,2],[5,3],[5,6],[2,4],[6,5],[5,0],[6,4],[5,6]],[[3,2],[4,2],[5,6],[5,4],[0,4],[5,6],[5,2],[5,2]],[[5,6],[0,5],[0,3],[5,1],[5,3],[2,5],[5,0],[5,3]]]
CAP = 15
YW = 15
def setup_inputs(rng):
    return {"x": rng.standard_normal((N, 128, T), dtype=np.float32).astype(ml_dtypes.bfloat16)}
def reference(x):
    y = np.full((N, 128, YW), np.nan, x.dtype)
    fill = [0] * N
    for r in range(N):
        for t in range(T):
            for e in ROUTE[r][t]:
                if fill[e] < CAP:
                    y[e][:, fill[e]] = x[r][:, t]
                fill[e] += 1
    return {"y": y}

@@ -1,0 +1,197 @@
+import comms_topo
+from concourse.bass import DstId, RemoteDMATransfer
+
+NR = 8
+SCRATCH = {
+    "xs": ("sbuf", [128, 8], "bfloat16"),
+    "ybuf": ("sbuf", [128, 15], "bfloat16"),
+    "xd": ("dram", [128, 8], "bfloat16"),
+    "land": ("dram", [8, 128, 8], "bfloat16"),
+}
+SEMAPHORES = ["lds", "ldd", "sent", "arr", "st", "gst", "gcp"] + ["a%d" % r for r in range(NR)]
+
+R_EXPERTS = (5,)
+R_PAIRS = ((1, 7),)
+R_WIDE = True
+DIRECT = (5,)
+GROUP = 8
+
+
+def way(r, e, k):
+    if e in R_EXPERTS or (r, e) in R_PAIRS or (R_WIDE and k >= 2 and r != e):
+        return "R"
+    return "S"
+
+
+def plan(tables):
+    route, cap = tables["ROUTE"], tables["CAP"]
+    fill = [0] * NR
+    kept = {}
+    for r in range(NR):
+        for t in range(len(route[r])):
+            for e in route[r][t]:
+                if fill[e] < cap:
+                    kept.setdefault((r, e), []).append((t, fill[e]))
+                fill[e] += 1
+    return kept
+
+
+def runs_of(kept, r, e, w):
+    out = []
+    for t, p in kept.get((r, e), []):
+        if out and out[-1][0] + out[-1][1] == t:
+            out[-1][1] += 1
+        else:
+            out.append([t, 1, p])
+    return [tuple(o) for o in out if way(r, e, o[1]) == w]
+
+
+def segments(runs):
+    segs = []
+    for t, k, p in runs:
+        if k == 1 and segs and segs[-1][4] and segs[-1][3] + segs[-1][2] == p:
+            t0, step, n, p0, _ = segs[-1]
+            if n == 1 or t0 + step * n == t:
+                segs[-1] = (t0, t - t0 if n == 1 else step, n + 1, p0, True)
+                continue
+        segs.append((t, 1, k, p, k == 1))
+    return [s[:4] for s in segs]
+
+
+def hops(a, b):
+    ca, cb = comms_topo.chip(a), comms_topo.chip(b)
+    return 1 if (comms_topo.mates(ca, cb) or comms_topo.same_plane(ca, cb)) else 2
+
+
+def s_calls(kept, r):
+    sruns = [(e, t, k, p) for e in range(NR) if e != r for (t, k, p) in runs_of(kept, r, e, "S")]
+    calls = []
+    for k in sorted(set(x[2] for x in sruns), reverse=True):
+        grp = [x for x in sruns if x[2] == k]
+        while grp:
+            part, grp = grp[:GROUP], grp[GROUP:]
+            slots = 1
+            while slots < len(part):
+                slots *= 2
+            ne = 8 // slots
+            calls.append([(e, t, kk, p, ((1 << ne) - 1) << (i * ne), ne) for i, (e, t, kk, p) in enumerate(part)])
+    return calls
+
+
+def rank_program(g, core, T, topo):
+    me = T.rank_of(core)
+    if me is None:
+        return
+    cores = T.cores
+    kept = plan(T.tables)
+    sem = T.sem
+
+    def did(e):
+        rid, pid, _ = topo.addr(cores[e])
+        return DstId(rid=rid, pnc=pid)
+
+    my_calls = s_calls(kept, me)
+    r_out = [e for e in range(NR) if e != me and runs_of(kept, me, e, "R")]
+    r_out.sort(key=lambda e: -hops(core, cores[e]))
+    self_s = runs_of(kept, me, me, "S")
+    self_r = runs_of(kept, me, me, "R")
+    need_xs = bool(my_calls) or bool(self_s)
+    arr_total = sum(c[5] for r in range(NR) if r != me for call in s_calls(kept, r) for c in call if c[0] == me)
+    r_in = [r for r in range(NR) if r != me and runs_of(kept, r, me, "R")]
+    r_in.sort(key=lambda r: hops(cores[r], core))
+    direct = me in DIRECT
+
+    cnt = {"st": 0, "gst": 0, "gcp": 0, "sent": 0, "arr": arr_total}
+    hw = [g.sync, g.scalar]
+    turn = [0]
+    waited = {0: set(), 1: set(), 2: set()}
+
+    def hwq(names):
+        i = turn[0] % 2
+        turn[0] += 1
+        for name, val in names:
+            if name not in waited[i]:
+                hw[i].wait_ge(sem[name], val)
+                waited[i].add(name)
+        return hw[i]
+
+    def gwait(name, val):
+        if name not in waited[2]:
+            g.wait_ge(sem[name], val)
+            waited[2].add(name)
+
+    if need_xs:
+        g.sync.dma_start(T.xs[:, :], T.x[:, :]).then_inc(sem.lds, 16)
+    if r_out:
+        g.scalar.dma_start(T.xd[:, :], T.x[:, :]).then_inc(sem.ldd, 16)
+
+    g_late = []
+    for (t, k, p) in self_s:
+        if "lds" not in waited[1]:
+            g.scalar.wait_ge(sem.lds, 16)
+            waited[1].add("lds")
+        g.scalar.dma_start(T.ybuf[:, p:p + k], T.xs[:, t:t + k]).then_inc(sem.arr, 16)
+        cnt["arr"] += 16
+    for (t, k, p) in self_r:
+        if k >= 2:
+            g.scalar.dma_start(T.y[:, p:p + k], T.x[:, t:t + k]).then_inc(sem.st, 16)
+            cnt["st"] += 16
+        else:
+            g_late.append((None, T.y[:, p:p + 1], T.x[:, t:t + 1], "gst"))
+
+    if r_out:
+        gwait("ldd", 16)
+        g.remote_dma_fused([RemoteDMATransfer(dst_ids=[did(e) for e in r_out], dma_engine_mask=0xFF,
+                                              remote_sem=sem["a%d" % me], srcs=[T.xd[:, :]],
+                                              dsts=[T.land[me] for e in r_out])], local_sem=sem.sent)
+        cnt["sent"] += 8
+    if my_calls:
+        gwait("lds", 16)
+        for call in my_calls:
+            g.remote_dma_fused([RemoteDMATransfer(dst_ids=[did(e)], dma_engine_mask=m, remote_sem=sem.arr,
+                                                  src=T.xs[:, t:t + k], dst=T.ybuf[:, p:p + k])
+                                for (e, t, k, p, m, ne) in call], local_sem=sem.sent)
+            cnt["sent"] += sum(c[5] for c in call)
+
+    tgt = T.y if direct else T.ybuf
+    for r in r_in:
+        for (t, step, n, p) in segments(runs_of(kept, r, me, "R")):
+            if step == 1 and n >= 2:
+                s = "st" if direct else "arr"
+                hwq([("a%d" % r, 8)]).dma_start(tgt[:, p:p + n], T.land[r, :, t:t + n]).then_inc(sem[s], 16)
+                cnt[s] += 16
+            else:
+                g_late.append(("a%d" % r, tgt[:, p:p + n], T.land[r, :, t:t + (n - 1) * step + 1:step],
+                               "gst" if direct else "gcp"))
+    for (name, out, in_, s) in g_late:
+        if name is not None:
+            gwait(name, 8)
+        g.dma_start(out, in_, allow_slow_non_contiguous=True).then_inc(sem[s], 16)
+        cnt[s] += 16
+
+    cols = sorted(p + i for r in range(NR) for w in ("S", "R") if w == "S" or (not direct and r != me)
+                  for (t, k, p) in runs_of(kept, r, me, w) for i in range(k))
+    pieces = []
+    for p in cols:
+        if pieces and pieces[-1][1] == p:
+            pieces[-1][1] = p + 1
+        else:
+            pieces.append([p, p + 1])
+    ready = [(n, cnt[n]) for n in ("arr", "gcp") if cnt[n]]
+    for a, b in pieces:
+        if b - a >= 2:
+            hwq(ready).dma_start(T.y[:, a:b], T.ybuf[:, a:b]).then_inc(sem.st, 16)
+            cnt["st"] += 16
+        else:
+            for n, v in ready:
+                gwait(n, v)
+            g.dma_start(T.y[:, a:b], T.ybuf[:, a:b], allow_slow_non_contiguous=True).then_inc(sem.gst, 16)
+            cnt["gst"] += 16
+
+    if need_xs:
+        gwait("lds", 16)
+    for r in r_in:
+        gwait("a%d" % r, 8)
+    for n in ("arr", "gcp", "sent", "gst", "st"):
+        if cnt[n]:
+            gwait(n, cnt[n])

@@ -8,17 +8,15 @@ SCRATCH = {
     "xd": ("dram", [128, 8], "bfloat16"),
     "land": ("dram", [8, 128, 8], "bfloat16"),
 }
-SEMAPHORES = ["lds", "ldd", "sent", "arr", "st", "gst", "gcp"] + ["a%d" % r for r in range(NR)]
+SEMAPHORES = ["lds", "ldd", "sent", "arr", "st", "gst"] + ["a%d" % r for r in range(NR)]
 
-R_EXPERTS = (5,)
-R_PAIRS = ((1, 7),)
-R_WIDE = True
-DIRECT = (5,)
-GROUP = 8
+R_WIDE = ((0, 1), (0, 5), (1, 5), (2, 5), (3, 0), (3, 4), (5, 3), (5, 6))
+R_ALL = ((0, 4), (1, 0), (1, 4), (1, 7), (2, 7), (2, 1), (4, 6), (4, 3), (5, 2), (7, 0), (7, 2), (7, 6),
+         (1, 1))
 
 
 def way(r, e, k):
-    if e in R_EXPERTS or (r, e) in R_PAIRS or (R_WIDE and k >= 2 and r != e):
+    if (r, e) in R_ALL or ((r, e) in R_WIDE and k >= 2):
         return "R"
     return "S"
 
@@ -65,16 +63,17 @@ def hops(a, b):
 
 def s_calls(kept, r):
     sruns = [(e, t, k, p) for e in range(NR) if e != r for (t, k, p) in runs_of(kept, r, e, "S")]
+    sruns.sort(key=lambda x: x[2])
     calls = []
-    for k in sorted(set(x[2] for x in sruns), reverse=True):
-        grp = [x for x in sruns if x[2] == k]
-        while grp:
-            part, grp = grp[:GROUP], grp[GROUP:]
-            slots = 1
-            while slots < len(part):
-                slots *= 2
-            ne = 8 // slots
-            calls.append([(e, t, kk, p, ((1 << ne) - 1) << (i * ne), ne) for i, (e, t, kk, p) in enumerate(part)])
+    while sruns:
+        part, sruns = sruns[:8], sruns[8:]
+        slots = 1
+        while slots < len(part):
+            slots *= 2
+        ne = 8 // slots
+        placed = [(e, t, k, p, ((1 << ne) - 1) << (i * ne), ne) for i, (e, t, k, p) in enumerate(part)]
+        for k in sorted(set(x[2] for x in placed)):
+            calls.append([x for x in placed if x[2] == k])
     return calls
 
 
@@ -99,20 +98,18 @@ def rank_program(g, core, T, topo):
     arr_total = sum(c[5] for r in range(NR) if r != me for call in s_calls(kept, r) for c in call if c[0] == me)
     r_in = [r for r in range(NR) if r != me and runs_of(kept, r, me, "R")]
     r_in.sort(key=lambda r: hops(cores[r], core))
-    direct = me in DIRECT
 
-    cnt = {"st": 0, "gst": 0, "gcp": 0, "sent": 0, "arr": arr_total}
+    cnt = {"st": 0, "gst": 0, "sent": 0, "arr": arr_total}
     hw = [g.sync, g.scalar]
     turn = [0]
     waited = {0: set(), 1: set(), 2: set()}
 
-    def hwq(names):
+    def hwq(name, val):
         i = turn[0] % 2
         turn[0] += 1
-        for name, val in names:
-            if name not in waited[i]:
-                hw[i].wait_ge(sem[name], val)
-                waited[i].add(name)
+        if name not in waited[i]:
+            hw[i].wait_ge(sem[name], val)
+            waited[i].add(name)
         return hw[i]
 
     def gwait(name, val):
@@ -125,7 +122,6 @@ def rank_program(g, core, T, topo):
     if r_out:
         g.scalar.dma_start(T.xd[:, :], T.x[:, :]).then_inc(sem.ldd, 16)
 
-    g_late = []
     for (t, k, p) in self_s:
         if "lds" not in waited[1]:
             g.scalar.wait_ge(sem.lds, 16)
@@ -137,7 +133,8 @@ def rank_program(g, core, T, topo):
             g.scalar.dma_start(T.y[:, p:p + k], T.x[:, t:t + k]).then_inc(sem.st, 16)
             cnt["st"] += 16
         else:
-            g_late.append((None, T.y[:, p:p + 1], T.x[:, t:t + 1], "gst"))
+            g.dma_start(T.y[:, p:p + 1], T.x[:, t:t + 1], allow_slow_non_contiguous=True).then_inc(sem.gst, 16)
+            cnt["gst"] += 16
 
     if r_out:
         gwait("ldd", 16)
@@ -153,38 +150,30 @@ def rank_program(g, core, T, topo):
                                 for (e, t, k, p, m, ne) in call], local_sem=sem.sent)
             cnt["sent"] += sum(c[5] for c in call)
 
-    tgt = T.y if direct else T.ybuf
     for r in r_in:
         for (t, step, n, p) in segments(runs_of(kept, r, me, "R")):
             if step == 1 and n >= 2:
-                s = "st" if direct else "arr"
-                hwq([("a%d" % r, 8)]).dma_start(tgt[:, p:p + n], T.land[r, :, t:t + n]).then_inc(sem[s], 16)
-                cnt[s] += 16
+                hwq("a%d" % r, 8).dma_start(T.y[:, p:p + n], T.land[r, :, t:t + n]).then_inc(sem.st, 16)
+                cnt["st"] += 16
             else:
-                g_late.append(("a%d" % r, tgt[:, p:p + n], T.land[r, :, t:t + (n - 1) * step + 1:step],
-                               "gst" if direct else "gcp"))
-    for (name, out, in_, s) in g_late:
-        if name is not None:
-            gwait(name, 8)
-        g.dma_start(out, in_, allow_slow_non_contiguous=True).then_inc(sem[s], 16)
-        cnt[s] += 16
+                gwait("a%d" % r, 8)
+                g.dma_start(T.y[:, p:p + n], T.land[r, :, t:t + (n - 1) * step + 1:step],
+                            allow_slow_non_contiguous=True).then_inc(sem.gst, 16)
+                cnt["gst"] += 16
 
-    cols = sorted(p + i for r in range(NR) for w in ("S", "R") if w == "S" or (not direct and r != me)
-                  for (t, k, p) in runs_of(kept, r, me, w) for i in range(k))
+    cols = sorted(p + i for r in range(NR) for (t, k, p) in runs_of(kept, r, me, "S") for i in range(k))
     pieces = []
     for p in cols:
         if pieces and pieces[-1][1] == p:
             pieces[-1][1] = p + 1
         else:
             pieces.append([p, p + 1])
-    ready = [(n, cnt[n]) for n in ("arr", "gcp") if cnt[n]]
     for a, b in pieces:
         if b - a >= 2:
-            hwq(ready).dma_start(T.y[:, a:b], T.ybuf[:, a:b]).then_inc(sem.st, 16)
+            hwq("arr", cnt["arr"]).dma_start(T.y[:, a:b], T.ybuf[:, a:b]).then_inc(sem.st, 16)
             cnt["st"] += 16
         else:
-            for n, v in ready:
-                gwait(n, v)
+            gwait("arr", cnt["arr"])
             g.dma_start(T.y[:, a:b], T.ybuf[:, a:b], allow_slow_non_contiguous=True).then_inc(sem.gst, 16)
             cnt["gst"] += 16
 
@@ -192,6 +181,6 @@ def rank_program(g, core, T, topo):
         gwait("lds", 16)
     for r in r_in:
         gwait("a%d" % r, 8)
-    for n in ("arr", "gcp", "sent", "gst", "st"):
+    for n in ("arr", "sent", "gst", "st"):
         if cnt[n]:
             gwait(n, cnt[n])

@@ -11,7 +11,7 @@ SCRATCH = {
 SEMAPHORES = ["lds", "ldd", "sent", "arr", "st", "gst"] + ["a%d" % r for r in range(NR)]
 
 R_WIDE = ((0, 1), (0, 5), (1, 5), (2, 5), (3, 0), (3, 4), (5, 3), (5, 6))
-R_ALL = ((0, 4), (1, 0), (1, 4), (1, 7), (2, 7), (2, 1), (4, 6), (4, 3), (5, 2), (7, 0), (7, 2), (7, 6),
+R_ALL = ((0, 4), (1, 0), (1, 4), (1, 7), (2, 7), (2, 1), (4, 6), (4, 3), (5, 2), (7, 0), (7, 1), (7, 2), (7, 6),
          (1, 1))
 
 
@@ -99,6 +99,7 @@ def rank_program(g, core, T, topo):
     r_in = [r for r in range(NR) if r != me and runs_of(kept, r, me, "R")]
     r_in.sort(key=lambda r: hops(cores[r], core))
 
+    count = sum(len(kept.get((r, me), [])) for r in range(NR))
     cnt = {"st": 0, "gst": 0, "sent": 0, "arr": arr_total}
     hw = [g.sync, g.scalar]
     turn = [0]
@@ -152,6 +153,8 @@ def rank_program(g, core, T, topo):
 
     for r in r_in:
         for (t, step, n, p) in segments(runs_of(kept, r, me, "R")):
+            if step == 1 and n == 1 and p == count - 1 and p + 2 <= T.tables["YW"] and t + 2 <= 8:
+                n = 2
             if step == 1 and n >= 2:
                 hwq("a%d" % r, 8).dma_start(T.y[:, p:p + n], T.land[r, :, t:t + n]).then_inc(sem.st, 16)
                 cnt["st"] += 16

@@ -8,11 +8,12 @@ SCRATCH = {
     "xd": ("dram", [128, 8], "bfloat16"),
     "land": ("dram", [8, 128, 8], "bfloat16"),
 }
-SEMAPHORES = ["lds", "ldd", "sent", "arr", "st", "gst"] + ["a%d" % r for r in range(NR)]
+SEMAPHORES = ["lds", "ldd", "sent", "arr", "st", "gst", "sf"] + ["a%d" % r for r in range(NR)]
 
 R_WIDE = ((0, 1), (0, 5), (1, 5), (2, 5), (3, 0), (3, 4), (5, 3), (5, 6))
 R_ALL = ((0, 4), (1, 0), (1, 4), (1, 7), (2, 7), (2, 1), (4, 6), (4, 3), (5, 2), (7, 0), (7, 1), (7, 2), (7, 6),
          (1, 1))
+WIDEN = {(4, 0, 1): (0, 2, 3), (4, 1, 2): (2, 2, 8), (4, 2, 0): (0, 2, 1)}
 
 
 def way(r, e, k):
@@ -63,6 +64,7 @@ def hops(a, b):
 
 def s_calls(kept, r):
     sruns = [(e, t, k, p) for e in range(NR) if e != r for (t, k, p) in runs_of(kept, r, e, "S")]
+    sruns = [(e,) + WIDEN.get((r, e, t), (t, k, p)) for (e, t, k, p) in sruns]
     sruns.sort(key=lambda x: x[2])
     calls = []
     while sruns:
@@ -98,9 +100,10 @@ def rank_program(g, core, T, topo):
     arr_total = sum(c[5] for r in range(NR) if r != me for call in s_calls(kept, r) for c in call if c[0] == me)
     r_in = [r for r in range(NR) if r != me and runs_of(kept, r, me, "R")]
     r_in.sort(key=lambda r: hops(cores[r], core))
+    wide_starts = [p for r in r_in for (t, k, p) in runs_of(kept, r, me, "R") if k >= 2]
 
     count = sum(len(kept.get((r, me), [])) for r in range(NR))
-    cnt = {"st": 0, "gst": 0, "sent": 0, "arr": arr_total}
+    cnt = {"st": 0, "gst": 0, "sent": 0, "arr": arr_total, "sf": 0}
     hw = [g.sync, g.scalar]
     turn = [0]
     waited = {0: set(), 1: set(), 2: set()}
@@ -108,9 +111,10 @@ def rank_program(g, core, T, topo):
     def hwq(name, val):
         i = turn[0] % 2
         turn[0] += 1
-        if name not in waited[i]:
-            hw[i].wait_ge(sem[name], val)
-            waited[i].add(name)
+        for nm, v in ((name, val), ("sf", cnt["sf"])):
+            if v and nm not in waited[i]:
+                hw[i].wait_ge(sem[nm], v)
+                waited[i].add(nm)
         return hw[i]
 
     def gwait(name, val):
@@ -123,19 +127,22 @@ def rank_program(g, core, T, topo):
     if r_out:
         g.scalar.dma_start(T.xd[:, :], T.x[:, :]).then_inc(sem.ldd, 16)
 
+    g_late = []
+    for (t, k, p) in self_r:
+        if k >= 2:
+            g.scalar.dma_start(T.y[:, p:p + k], T.x[:, t:t + k]).then_inc(sem.st, 16)
+            cnt["st"] += 16
+        elif p + 1 in wide_starts and t + 2 <= 8:
+            g.scalar.dma_start(T.y[:, p:p + 2], T.x[:, t:t + 2]).then_inc(sem.sf, 16)
+            cnt["sf"] += 16
+        else:
+            g_late.append((T.y[:, p:p + 1], T.x[:, t:t + 1]))
     for (t, k, p) in self_s:
         if "lds" not in waited[1]:
             g.scalar.wait_ge(sem.lds, 16)
             waited[1].add("lds")
         g.scalar.dma_start(T.ybuf[:, p:p + k], T.xs[:, t:t + k]).then_inc(sem.arr, 16)
         cnt["arr"] += 16
-    for (t, k, p) in self_r:
-        if k >= 2:
-            g.scalar.dma_start(T.y[:, p:p + k], T.x[:, t:t + k]).then_inc(sem.st, 16)
-            cnt["st"] += 16
-        else:
-            g.dma_start(T.y[:, p:p + 1], T.x[:, t:t + 1], allow_slow_non_contiguous=True).then_inc(sem.gst, 16)
-            cnt["gst"] += 16
 
     if r_out:
         gwait("ldd", 16)
@@ -150,6 +157,9 @@ def rank_program(g, core, T, topo):
                                                   src=T.xs[:, t:t + k], dst=T.ybuf[:, p:p + k])
                                 for (e, t, k, p, m, ne) in call], local_sem=sem.sent)
             cnt["sent"] += sum(c[5] for c in call)
+    for (out, in_) in g_late:
+        g.dma_start(out, in_, allow_slow_non_contiguous=True).then_inc(sem.gst, 16)
+        cnt["gst"] += 16
 
     for r in r_in:
         for (t, step, n, p) in segments(runs_of(kept, r, me, "R")):
@@ -184,6 +194,6 @@ def rank_program(g, core, T, topo):
         gwait("lds", 16)
     for r in r_in:
         gwait("a%d" % r, 8)
-    for n in ("arr", "sent", "gst", "st"):
+    for n in ("sf", "arr", "sent", "gst", "st"):
         if cnt[n]:
             gwait(n, cnt[n])

import comms_topo
from concourse.bass import DstId, RemoteDMATransfer

NR = 8
SCRATCH = {
    "xs": ("sbuf", [128, 8], "bfloat16"),
    "ybuf": ("sbuf", [128, 15], "bfloat16"),
    "xd": ("dram", [128, 8], "bfloat16"),
    "land": ("dram", [8, 128, 8], "bfloat16"),
}
SEMAPHORES = ["lds", "ldd", "sent", "arr", "st", "gst", "sf"] + ["a%d" % r for r in range(NR)]

R_WIDE = ((0, 1), (0, 5), (1, 5), (2, 5), (3, 0), (3, 4), (5, 3), (5, 6))
R_ALL = ((0, 4), (1, 0), (1, 4), (1, 7), (2, 7), (2, 1), (4, 6), (4, 3), (5, 2), (7, 0), (7, 1), (7, 2), (7, 6),
         (1, 1))
WIDEN = {(4, 0, 1): (0, 2, 3), (4, 1, 2): (2, 2, 8), (4, 2, 0): (0, 2, 1)}


def way(r, e, k):
    if (r, e) in R_ALL or ((r, e) in R_WIDE and k >= 2):
        return "R"
    return "S"


def plan(tables):
    route, cap = tables["ROUTE"], tables["CAP"]
    fill = [0] * NR
    kept = {}
    for r in range(NR):
        for t in range(len(route[r])):
            for e in route[r][t]:
                if fill[e] < cap:
                    kept.setdefault((r, e), []).append((t, fill[e]))
                fill[e] += 1
    return kept


def runs_of(kept, r, e, w):
    out = []
    for t, p in kept.get((r, e), []):
        if out and out[-1][0] + out[-1][1] == t:
            out[-1][1] += 1
        else:
            out.append([t, 1, p])
    return [tuple(o) for o in out if way(r, e, o[1]) == w]


def segments(runs):
    segs = []
    for t, k, p in runs:
        if k == 1 and segs and segs[-1][4] and segs[-1][3] + segs[-1][2] == p:
            t0, step, n, p0, _ = segs[-1]
            if n == 1 or t0 + step * n == t:
                segs[-1] = (t0, t - t0 if n == 1 else step, n + 1, p0, True)
                continue
        segs.append((t, 1, k, p, k == 1))
    return [s[:4] for s in segs]


def hops(a, b):
    ca, cb = comms_topo.chip(a), comms_topo.chip(b)
    return 1 if (comms_topo.mates(ca, cb) or comms_topo.same_plane(ca, cb)) else 2


def s_calls(kept, r):
    sruns = [(e, t, k, p) for e in range(NR) if e != r for (t, k, p) in runs_of(kept, r, e, "S")]
    sruns = [(e,) + WIDEN.get((r, e, t), (t, k, p)) for (e, t, k, p) in sruns]
    sruns.sort(key=lambda x: x[2])
    calls = []
    while sruns:
        part, sruns = sruns[:8], sruns[8:]
        slots = 1
        while slots < len(part):
            slots *= 2
        ne = 8 // slots
        placed = [(e, t, k, p, ((1 << ne) - 1) << (i * ne), ne) for i, (e, t, k, p) in enumerate(part)]
        for k in sorted(set(x[2] for x in placed)):
            calls.append([x for x in placed if x[2] == k])
    return calls


def rank_program(g, core, T, topo):
    me = T.rank_of(core)
    if me is None:
        return
    cores = T.cores
    kept = plan(T.tables)
    sem = T.sem

    def did(e):
        rid, pid, _ = topo.addr(cores[e])
        return DstId(rid=rid, pnc=pid)

    my_calls = s_calls(kept, me)
    r_out = [e for e in range(NR) if e != me and runs_of(kept, me, e, "R")]
    r_out.sort(key=lambda e: -hops(core, cores[e]))
    self_s = runs_of(kept, me, me, "S")
    self_r = runs_of(kept, me, me, "R")
    need_xs = bool(my_calls) or bool(self_s)
    arr_total = sum(c[5] for r in range(NR) if r != me for call in s_calls(kept, r) for c in call if c[0] == me)
    r_in = [r for r in range(NR) if r != me and runs_of(kept, r, me, "R")]
    r_in.sort(key=lambda r: hops(cores[r], core))
    wide_starts = [p for r in r_in for (t, k, p) in runs_of(kept, r, me, "R") if k >= 2]

    count = sum(len(kept.get((r, me), [])) for r in range(NR))
    cnt = {"st": 0, "gst": 0, "sent": 0, "arr": arr_total, "sf": 0}
    hw = [g.sync, g.scalar]
    turn = [0]
    waited = {0: set(), 1: set(), 2: set()}

    def hwq(name, val):
        i = turn[0] % 2
        turn[0] += 1
        for nm, v in ((name, val), ("sf", cnt["sf"])):
            if v and nm not in waited[i]:
                hw[i].wait_ge(sem[nm], v)
                waited[i].add(nm)
        return hw[i]

    def gwait(name, val):
        if name not in waited[2]:
            g.wait_ge(sem[name], val)
            waited[2].add(name)

    if need_xs:
        g.sync.dma_start(T.xs[:, :], T.x[:, :]).then_inc(sem.lds, 16)
    if r_out:
        g.scalar.dma_start(T.xd[:, :], T.x[:, :]).then_inc(sem.ldd, 16)

    g_late = []
    for (t, k, p) in self_r:
        if k >= 2:
            g.scalar.dma_start(T.y[:, p:p + k], T.x[:, t:t + k]).then_inc(sem.st, 16)
            cnt["st"] += 16
        elif p + 1 in wide_starts and t + 2 <= 8:
            g.scalar.dma_start(T.y[:, p:p + 2], T.x[:, t:t + 2]).then_inc(sem.sf, 16)
            cnt["sf"] += 16
        else:
            g_late.append((T.y[:, p:p + 1], T.x[:, t:t + 1]))
    for (t, k, p) in self_s:
        if "lds" not in waited[1]:
            g.scalar.wait_ge(sem.lds, 16)
            waited[1].add("lds")
        g.scalar.dma_start(T.ybuf[:, p:p + k], T.xs[:, t:t + k]).then_inc(sem.arr, 16)
        cnt["arr"] += 16

    if r_out:
        gwait("ldd", 16)
        g.remote_dma_fused([RemoteDMATransfer(dst_ids=[did(e) for e in r_out], dma_engine_mask=0xFF,
                                              remote_sem=sem["a%d" % me], srcs=[T.xd[:, :]],
                                              dsts=[T.land[me] for e in r_out])], local_sem=sem.sent)
        cnt["sent"] += 8
    if my_calls:
        gwait("lds", 16)
        for call in my_calls:
            g.remote_dma_fused([RemoteDMATransfer(dst_ids=[did(e)], dma_engine_mask=m, remote_sem=sem.arr,
                                                  src=T.xs[:, t:t + k], dst=T.ybuf[:, p:p + k])
                                for (e, t, k, p, m, ne) in call], local_sem=sem.sent)
            cnt["sent"] += sum(c[5] for c in call)
    for (out, in_) in g_late:
        g.dma_start(out, in_, allow_slow_non_contiguous=True).then_inc(sem.gst, 16)
        cnt["gst"] += 16

    for r in r_in:
        for (t, step, n, p) in segments(runs_of(kept, r, me, "R")):
            if step == 1 and n == 1 and p == count - 1 and p + 2 <= T.tables["YW"] and t + 2 <= 8:
                n = 2
            if step == 1 and n >= 2:
                hwq("a%d" % r, 8).dma_start(T.y[:, p:p + n], T.land[r, :, t:t + n]).then_inc(sem.st, 16)
                cnt["st"] += 16
            else:
                gwait("a%d" % r, 8)
                g.dma_start(T.y[:, p:p + n], T.land[r, :, t:t + (n - 1) * step + 1:step],
                            allow_slow_non_contiguous=True).then_inc(sem.gst, 16)
                cnt["gst"] += 16

    cols = sorted(p + i for r in range(NR) for (t, k, p) in runs_of(kept, r, me, "S") for i in range(k))
    pieces = []
    for p in cols:
        if pieces and pieces[-1][1] == p:
            pieces[-1][1] = p + 1
        else:
            pieces.append([p, p + 1])
    for a, b in pieces:
        if b - a >= 2:
            hwq("arr", cnt["arr"]).dma_start(T.y[:, a:b], T.ybuf[:, a:b]).then_inc(sem.st, 16)
            cnt["st"] += 16
        else:
            gwait("arr", cnt["arr"])
            g.dma_start(T.y[:, a:b], T.ybuf[:, a:b], allow_slow_non_contiguous=True).then_inc(sem.gst, 16)
            cnt["gst"] += 16

    if need_xs:
        gwait("lds", 16)
    for r in r_in:
        gwait("a%d" % r, 8)
    for n in ("sf", "arr", "sent", "gst", "st"):
        if cnt[n]:
            gwait(n, cnt[n])
